import numpy as np
import ml_dtypes


def mxq(x, axis, fmt="e4m3"):
    dtype, down = {"e4m3": (ml_dtypes.float8_e4m3fn, 7), "e5m2": (ml_dtypes.float8_e5m2, 14)}[fmt]
    v = np.moveaxis(np.asarray(x, np.float32).astype(ml_dtypes.bfloat16).astype(np.float64), axis, -1)
    blocks = v.reshape(v.shape[:-1] + (-1, 32))
    amax = np.abs(blocks).max(-1, keepdims=True)
    byte = np.maximum(np.where(amax > 0, np.frexp(amax)[1] - 1 + 127, 0) - down, 1)
    scale = np.exp2(byte - 127.0)
    codes = (blocks / scale).astype(np.float32).astype(dtype).astype(np.float64)
    return np.moveaxis((codes * scale).reshape(v.shape), -1, axis)


WIDE = False


def mx_kscale(k):
    if not WIDE:
        return np.ones(k)
    levels = np.array([30, -30])
    if k % 512:
        return np.exp2(np.random.permutation(np.resize(levels, k // 32))).repeat(32)
    a = np.empty((k // 512, 16))
    for p in range(k // 512):
        a[p, :8] = np.random.permutation(np.resize(levels, 8))
        for g in range(8):
            far = levels[np.abs(levels - a[p, g]) >= 10]
            a[p, g + 8] = far[np.random.randint(len(far))]
    return np.exp2(a.ravel()).repeat(32)


def f64(x):
    return np.asarray(x).astype(np.float64)


def striped(idx):
    return np.tile(np.asarray(idx).reshape(-1, 16).T, (8, 1)).astype(np.uint16)


def unstriped(offs):
    return offs[:16].T.reshape(-1).astype(np.int64)


E2M1 = np.array([0.0, 0.5, 1.0, 1.5, 2.0, 3.0, 4.0, 6.0, -0.0, -0.5, -1.0, -1.5, -2.0, -3.0, -4.0, -6.0])


def pack_weight(w, fmt):
    k, n = w.shape
    w = f64(np.asarray(w, np.float32).astype(ml_dtypes.bfloat16)).reshape(k // 32, 32, n)
    amax = np.abs(w).max(1)
    if fmt in ("e4m3", "e5m2"):
        byte = np.frexp(amax)[1] - 1 + 127 - (7 if fmt == "e4m3" else 14)
    else:
        mant, ex = np.frexp(amax / 6.0)
        byte = np.where(mant > 0.5, ex, ex - 1) + 127
    byte = np.clip(np.where(amax > 0, byte, 1), 1, 254)
    scaled = (w * np.exp2(127.0 - byte)[:, None, :]).reshape(k, n).astype(np.float32)
    by_word = np.ascontiguousarray(scaled.reshape(k // 512, 128, 4, n).transpose(0, 1, 3, 2))
    if fmt in ("e4m3", "e5m2"):
        words = by_word.astype(ml_dtypes.float8_e4m3fn if fmt == "e4m3" else ml_dtypes.float8_e5m2).view(np.uint8)
    else:
        c = by_word.astype(ml_dtypes.float4_e2m1fn).view(np.uint8) & 0xF
        words = (c[..., 0::2] | (c[..., 1::2] << 4)).reshape(k // 512, 128, 2 * n)
    return np.ascontiguousarray(words), np.ascontiguousarray(byte.astype(np.uint8).reshape(k // 512, 16, n))


def unpack_weight(words, scales, fmt):
    g, _, n = scales.shape
    words = np.ascontiguousarray(words).reshape(g, 128, n, -1)
    if fmt in ("e4m3", "e5m2"):
        vals = words.view(ml_dtypes.float8_e4m3fn if fmt == "e4m3" else ml_dtypes.float8_e5m2).astype(np.float64)
    else:
        nib = np.empty((g, 128, n, 4), np.uint8)
        nib[..., 0::2] = words & 0xF
        nib[..., 1::2] = words >> 4
        vals = E2M1[nib]
    vals = vals * np.repeat(np.exp2(scales.astype(np.float64) - 127.0), 8, axis=1)[..., None]
    return vals.transpose(0, 1, 3, 2).reshape(g * 512, n)


K, T, J, R, V, N = 512, 1024, 256, 512, 1024, 256


def setup_inputs():
    n = np.random.standard_normal
    idx = np.random.permutation(T)[:J]
    idx2 = np.random.permutation(V)[:J]
    idx3 = np.random.permutation(T)[:J]
    fk = mx_kscale(K)
    fr = mx_kscale(R)
    xtp = pack_weight(n((K, T)) / fk[:, None], "e5m2")
    wp = pack_weight(n((K, R)) * 1 / np.sqrt(K) * fk[:, None] * fr, "e2m1")
    w2p = pack_weight(n((K, R)) * 1 / np.sqrt(K) * fk[:, None] * fr, "e4m3")
    wbp = pack_weight(n((R, N)) * 1 / np.sqrt(R) / fr[:, None], "e2m1")
    wsp = pack_weight(n((K, N)) * 1 / np.sqrt(K) * fk[:, None], "e2m1")
    return {
        "xt_words": xtp[0],
        "xt_scales": xtp[1],
        "w_words": wp[0],
        "w_scales": wp[1],
        "w2_words": w2p[0],
        "w2_scales": w2p[1],
        "tb": (np.random.randint(-9, 10, (R, V)).astype(np.float64)).astype(np.float32),
        "st": (np.random.uniform(0.08, 0.3, (R, 1))).astype(np.float32),
        "wb_words": wbp[0],
        "wb_scales": wbp[1],
        "ws_words": wsp[0],
        "ws_scales": wsp[1],
        "offs": striped(idx),
        "offs2": striped(idx2),
        "offs3": striped(idx3),
    }


def reference(xt_words, xt_scales, w_words, w_scales, w2_words, w2_scales, tb, st, wb_words, wb_scales, ws_words, ws_scales, offs, offs2, offs3):
    idx = unstriped(offs)
    idx2 = unstriped(offs2)
    idx3 = unstriped(offs3)
    xtu = unpack_weight(xt_words, xt_scales, "e5m2")
    wu = unpack_weight(w_words, w_scales, "e2m1")
    w2u = unpack_weight(w2_words, w2_scales, "e4m3")
    wbu = unpack_weight(wb_words, wb_scales, "e2m1")
    wsu = unpack_weight(ws_words, ws_scales, "e2m1")
    xtidxg = xtu[:, idx]
    a = wu.T @ xtidxg
    b = w2u.T @ xtidxg
    hid = np.maximum(a * f64(tb)[:, idx2] * f64(st), b)
    hidq = mxq(hid, 0, "e4m3")
    xtidx3g = xtu[:, idx3]
    y = wbu.T @ hidq + wsu.T @ xtidx3g
    return y

@@ -1,0 +1,192 @@
+from contextlib import ExitStack
+
+import concourse.mybir as mybir
+
+K, T, J, R, V, N = 512, 1024, 256, 512, 1024, 256
+FLOPS = 2 * (2 * K * R * J + R * N * J + K * N * J)
+
+F32 = mybir.dt.float32
+BF16 = mybir.dt.bfloat16
+I32 = mybir.dt.int32
+U32 = mybir.dt.uint32
+U16 = mybir.dt.uint16
+U8 = mybir.dt.uint8
+E4M3 = mybir.dt.float8_e4m3fn_x4
+E5M2 = mybir.dt.float8_e5m2_x4
+E2M1 = mybir.dt.float4_e2m1fn_x4
+ALU = mybir.AluOpType
+COPY = mybir.ActivationFunctionType.Copy
+
+P = 128
+PACK = 4
+HALF = J // 2
+
+
+def tile_list_gaintable_twow_further_plain_kernel(
+    tc, xt_words, xt_scales, w_words, w_scales, w2_words, w2_scales, tb, st,
+    wb_words, wb_scales, ws_words, ws_scales, offs, offs2, offs3, out,
+):
+    nc = tc.nc
+    with ExitStack() as ctx:
+        sb = ctx.enter_context(tc.tile_pool(name="sb", bufs=1))
+        ps = ctx.enter_context(tc.psum_pool(name="ps", bufs=1))
+
+        def tile(name, shape, dtype):
+            return sb.tile(shape, dtype, name=name, align_bytes=64)
+
+        def scale_rows(scales):
+            return scales[0].bitcast(I32).rearrange("(q r) c -> r q c", r=4)
+
+        def spread(plane, stage):
+            for q in range(4):
+                nc.vector.tensor_copy(out=plane[32 * q : 32 * q + 4, :].bitcast(I32), in_=stage[:, q, :])
+
+        o1 = tile("o1", [P, J // 16], U16)
+        o2 = tile("o2", [P, J // 16], U16)
+        o3 = tile("o3", [P, J // 16], U16)
+        xw = tile("xw", [P, T], U32)
+        xs_stage = tile("xs_stage", [4, 4, T // 4], I32)
+        xs = tile("xs", [P, T], U8)
+        w_raw = tile("w_raw", [P, 2 * R], U8)
+        w2_raw = tile("w2_raw", [P, R], U32)
+        up_stage = tile("up_stage", [4, 4, 2 * R // 4], I32)
+        up_raw = tile("up_raw", [P, 2 * R], U8)
+        dn_stage = tile("dn_stage", [4, 4, 2 * N // 4], I32)
+        dn_sc = tile("dn_sc", [P, 2 * N], U8)
+        wb_w = tile("wb_w", [P, 2 * N], U8)
+        ws_w = tile("ws_w", [P, 2 * N], U8)
+        st_sb = tile("st_sb", [P, PACK], F32)
+        tbs = [tile("tb%d" % t, [P, V], F32) for t in range(PACK)]
+        tb_rows = tb.rearrange("(p t) v -> t p v", t=PACK)
+
+        nc.sync.dma_start(o1[:], offs)
+        nc.scalar.dma_start(xw[:].bitcast(I32), xt_words[0].rearrange("p n t -> p (n t)").bitcast(I32))
+        nc.sync.dma_start(xs_stage[:], scale_rows(xt_scales))
+        nc.scalar.dma_start(w_raw[:].bitcast(I32), w_words[0].bitcast(I32))
+        nc.sync.dma_start(up_stage[:, :, 0 : R // 4], scale_rows(w_scales))
+        nc.scalar.dma_start(w2_raw[:].bitcast(I32), w2_words[0].rearrange("p n t -> p (n t)").bitcast(I32))
+        nc.sync.dma_start(up_stage[:, :, R // 4 : 2 * R // 4], scale_rows(w2_scales))
+        nc.sync.dma_start(o2[:], offs2)
+        nc.sync.dma_start(tbs[0][:], tb_rows[0])
+        nc.sync.dma_start(st_sb[:], st.rearrange("(p t) o -> p (t o)", t=PACK))
+        nc.sync.dma_start(tbs[1][:], tb_rows[1])
+        nc.sync.dma_start(o3[:], offs3)
+        nc.sync.dma_start(tbs[2][:], tb_rows[2])
+        nc.sync.dma_start(dn_stage[:, :, 0 : N // 4], scale_rows(ws_scales))
+        nc.sync.dma_start(dn_stage[:, :, N // 4 : 2 * N // 4], scale_rows(wb_scales))
+        nc.sync.dma_start(tbs[3][:], tb_rows[3])
+        nc.sync.dma_start(ws_w[:].bitcast(I32), ws_words[0].bitcast(I32))
+        nc.sync.dma_start(wb_w[:].bitcast(I32), wb_words[0].bitcast(I32))
+
+        nc.vector.memset(xs[:].bitcast(U32), 0)
+        nc.vector.memset(up_raw[:].bitcast(U32), 0)
+        nc.vector.memset(dn_sc[:].bitcast(U32), 0)
+
+        spread(xs, xs_stage)
+        spread(up_raw, up_stage)
+
+        xg_s = tile("xg_s", [P, J], U8)
+        xg_w = tile("xg_w", [P, J], U32)
+        nc.vector.tensor_copy(out=xg_s[:], in_=xs[:].indirect(o1[:]))
+        up_sc = tile("up_sc", [P, 2, R], U8)
+        for a in range(2):
+            nc.vector.tensor_copy(
+                out=up_sc[:, a, :].rearrange("p (t c i) -> p c t i", t=PACK, i=16),
+                in_=up_raw[:, a * R : (a + 1) * R].rearrange("p (c i t) -> p c t i", t=PACK, i=16),
+            )
+        nc.vector.tensor_copy(out=xg_w[:], in_=xw[:].indirect(o1[:]))
+
+        w_p = tile("w_p", [P, 2 * R], U8)
+        w2_p = tile("w2_p", [P, R], U32)
+        nc.scalar.copy(
+            out=w_p[:].bitcast(U16).rearrange("p (t c i) -> p c t i", t=PACK, i=8),
+            in_=w_raw[:].bitcast(U16).rearrange("p (c i t) -> p c t i", t=PACK, i=8),
+        )
+        nc.scalar.copy(
+            out=w2_p[:].rearrange("p (t c i) -> p c t i", t=PACK, i=4),
+            in_=w2_raw[:].rearrange("p (c i t) -> p c t i", t=PACK, i=4),
+        )
+
+        a_ps = [ps.tile([P, 2, J], F32, name="a%d" % u) for u in range(2)]
+        b_ps = [ps.tile([P, PACK, HALF], F32, name="b%d" % h) for h in range(2)]
+        y_ps = [[ps.tile([P, HALF], F32, name="y%d%d" % (h, u)) for u in range(2)] for h in range(2)]
+        for t in range(PACK):
+            nc.tensor.matmul_mx(
+                out=a_ps[t // 2][:, t % 2, :],
+                lhsT=w_p[:, 2 * P * t : 2 * P * (t + 1)].bitcast(E2M1),
+                lhsT_scale=up_sc[:, 0, P * t : P * (t + 1)],
+                rhs=xg_w[:].bitcast(E5M2), rhs_scale=xg_s[:], start=True, stop=True,
+            )
+        for h in range(2):
+            js = slice(h * HALF, (h + 1) * HALF)
+            for t in range(PACK):
+                nc.tensor.matmul_mx(
+                    out=b_ps[h][:, t, :],
+                    lhsT=w2_p[:, P * t : P * (t + 1)].bitcast(E4M3),
+                    lhsT_scale=up_sc[:, 1, P * t : P * (t + 1)],
+                    rhs=xg_w[:, js].bitcast(E5M2), rhs_scale=xg_s[:, js], start=True, stop=True,
+                )
+
+        x3_s = tile("x3_s", [P, J], U8)
+        x3_w = tile("x3_w", [P, J], U32)
+        nc.vector.tensor_copy(out=x3_s[:], in_=xs[:].indirect(o3[:]))
+        nc.vector.tensor_copy(out=x3_w[:], in_=xw[:].indirect(o3[:]))
+        spread(dn_sc, dn_stage)
+        for h in range(2):
+            js = slice(h * HALF, (h + 1) * HALF)
+            for u in range(2):
+                nc.tensor.matmul_mx(
+                    out=y_ps[h][u][:],
+                    lhsT=ws_w[:, 2 * P * u : 2 * P * (u + 1)].bitcast(E2M1),
+                    lhsT_scale=dn_sc[:, P * u : P * (u + 1)],
+                    rhs=x3_w[:, js].bitcast(E5M2), rhs_scale=x3_s[:, js], start=True, stop=False,
+                )
+
+        gains = tile("gains", [P, PACK, J], F32)
+        prod = tile("prod", [P, 2, PACK, HALF], F32)
+        for t in range(PACK - 1):
+            nc.scalar.activation(out=gains[:, t, :], in_=tbs[t][:].indirect(o2[:]), func=COPY, scale=st_sb[:, t : t + 1])
+            nc.vector.tensor_tensor(
+                out=prod[:, :, t, :],
+                in0=a_ps[t // 2][:, t % 2, :].rearrange("p (h j) -> p h j", h=2),
+                in1=gains[:, t, :].rearrange("p (h j) -> p h j", h=2),
+                op=ALU.mult,
+            )
+        t = PACK - 1
+        for h in range(2):
+            js = slice(h * HALF, (h + 1) * HALF)
+            nc.scalar.activation(
+                out=gains[:, t, js], in_=tbs[t][:].indirect(o2[:, 8 * h : 8 * (h + 1)]), func=COPY, scale=st_sb[:, t : t + 1]
+            )
+            nc.vector.tensor_tensor(out=prod[:, h, t, :], in0=a_ps[t // 2][:, t % 2, js], in1=gains[:, t, js], op=ALU.mult)
+
+        hid = [tile("hid%d" % h, [P, HALF, PACK], BF16) for h in range(2)]
+        hq_w = [tile("hq_w%d" % h, [P, HALF], U32) for h in range(2)]
+        hq_s = [tile("hq_s%d" % h, [P, HALF], U8) for h in range(2)]
+        for h in range(2):
+            nc.vector.tensor_tensor(
+                out=hid[h][:].rearrange("p (c i) t -> p c t i", i=2),
+                in0=b_ps[h][:].rearrange("p t (c i) -> p c t i", i=2),
+                in1=prod[:, h].rearrange("p t (c i) -> p c t i", i=2),
+                op=ALU.max,
+            )
+        res = [tile("res%d" % h, [P, 2, HALF], F32) for h in range(2)]
+        out_v = out.rearrange("(u p) j -> p u j", p=P)
+        for h in range(2):
+            js = slice(h * HALF, (h + 1) * HALF)
+            nc.vector.quantize_mx(out=hq_w[h][:].bitcast(E4M3), scales=hq_s[h][:], in_=hid[h][:].rearrange("p j t -> p (j t)"))
+            for u in range(2):
+                nc.tensor.matmul_mx(
+                    out=y_ps[h][u][:],
+                    lhsT=wb_w[:, 2 * P * u : 2 * P * (u + 1)].bitcast(E2M1),
+                    lhsT_scale=dn_sc[:, N + P * u : N + P * (u + 1)],
+                    rhs=hq_w[h][:].bitcast(E4M3), rhs_scale=hq_s[h][:], start=False, stop=True,
+                )
+        for h in range(2):
+            js = slice(h * HALF, (h + 1) * HALF)
+            nc.scalar.copy(out=res[h][:, 0, :], in_=y_ps[h][0][:])
+            if h == 0:
+                nc.scalar.copy(out=res[h][:, 1, :], in_=y_ps[h][1][:])
+            else:
+                nc.vector.tensor_copy(out=res[h][:, 1, :], in_=y_ps[h][1][:])
+            nc.sync.dma_start(out_v[:, :, js], res[h][:])

@@ -37,6 +37,18 @@ def tile_list_gaintable_twow_further_plain_kernel(
         def scale_rows(scales):
             return scales[0].bitcast(I32).rearrange("(q r) c -> r q c", r=4)
 
+        def load_split(queue_lo, queue_hi, stage, scales):
+            rows = scale_rows(scales)
+            return [
+                lambda: queue_lo.dma_start(stage[0:4], rows[:, 0:2, :]),
+                lambda: queue_hi.dma_start(stage[64:68], rows[:, 2:4, :]),
+            ]
+
+        def spread_split(plane, stage):
+            for q in range(4):
+                base = 64 * (q // 2)
+                nc.vector.tensor_copy(out=plane[32 * q : 32 * q + 4, :].bitcast(I32), in_=stage[base : base + 4, q % 2, :])
+
         def spread(plane, stage):
             for q in range(4):
                 nc.vector.tensor_copy(out=plane[32 * q : 32 * q + 4, :].bitcast(I32), in_=stage[:, q, :])
@@ -45,12 +57,14 @@ def tile_list_gaintable_twow_further_plain_kernel(
         o2 = tile("o2", [P, J // 16], U16)
         o3 = tile("o3", [P, J // 16], U16)
         xw = tile("xw", [P, T], U32)
-        xs_stage = tile("xs_stage", [4, 4, T // 4], I32)
+        xs_stage = tile("xs_stage", [P, 2, T // 4], I32)
         xs = tile("xs", [P, T], U8)
         w_raw = tile("w_raw", [P, 2 * R], U8)
         w2_raw = tile("w2_raw", [P, R], U32)
-        up_stage = tile("up_stage", [4, 4, 2 * R // 4], I32)
-        up_raw = tile("up_raw", [P, 2 * R], U8)
+        w_stage = tile("w_stage", [P, 2, R // 4], I32)
+        w2_stage = tile("w2_stage", [P, 2, R // 4], I32)
+        w_sraw = tile("w_sraw", [P, R], U8)
+        w2_sraw = tile("w2_sraw", [P, R], U8)
         dn_stage = tile("dn_stage", [4, 4, 2 * N // 4], I32)
         dn_sc = tile("dn_sc", [P, 2 * N], U8)
         wb_w = tile("wb_w", [P, 2 * N], U8)
@@ -59,15 +73,21 @@ def tile_list_gaintable_twow_further_plain_kernel(
         tbs = [tile("tb%d" % t, [P, V], F32) for t in range(PACK)]
         tb_rows = tb.rearrange("(p t) v -> t p v", t=PACK)
 
+        xs_load = load_split(nc.scalar, nc.sync, xs_stage, xt_scales)
+        w_load = load_split(nc.sync, nc.sync, w_stage, w_scales)
+        w2_load = load_split(nc.sync, nc.sync, w2_stage, w2_scales)
         nc.sync.dma_start(o1[:], offs)
+        xs_load[0]()
+        xs_load[1]()
         nc.scalar.dma_start(xw[:].bitcast(I32), xt_words[0].rearrange("p n t -> p (n t)").bitcast(I32))
-        nc.sync.dma_start(xs_stage[:], scale_rows(xt_scales))
+        w_load[0]()
         nc.scalar.dma_start(w_raw[:].bitcast(I32), w_words[0].bitcast(I32))
-        nc.sync.dma_start(up_stage[:, :, 0 : R // 4], scale_rows(w_scales))
+        w_load[1]()
         nc.scalar.dma_start(w2_raw[:].bitcast(I32), w2_words[0].rearrange("p n t -> p (n t)").bitcast(I32))
-        nc.sync.dma_start(up_stage[:, :, R // 4 : 2 * R // 4], scale_rows(w2_scales))
-        nc.sync.dma_start(o2[:], offs2)
         nc.sync.dma_start(tbs[0][:], tb_rows[0])
+        w2_load[0]()
+        w2_load[1]()
+        nc.sync.dma_start(o2[:], offs2)
         nc.sync.dma_start(st_sb[:], st.rearrange("(p t) o -> p (t o)", t=PACK))
         nc.sync.dma_start(tbs[1][:], tb_rows[1])
         nc.sync.dma_start(o3[:], offs3)
@@ -78,23 +98,27 @@ def tile_list_gaintable_twow_further_plain_kernel(
         nc.sync.dma_start(ws_w[:].bitcast(I32), ws_words[0].bitcast(I32))
         nc.sync.dma_start(wb_w[:].bitcast(I32), wb_words[0].bitcast(I32))
 
-        nc.vector.memset(xs[:].bitcast(U32), 0)
-        nc.vector.memset(up_raw[:].bitcast(U32), 0)
-        nc.vector.memset(dn_sc[:].bitcast(U32), 0)
-
-        spread(xs, xs_stage)
-        spread(up_raw, up_stage)
+        for plane in (xs, w_sraw, w2_sraw, dn_sc):
+            nc.vector.memset(plane[:].bitcast(U32), 0)
 
         xg_s = tile("xg_s", [P, J], U8)
         xg_w = tile("xg_w", [P, J], U32)
-        nc.vector.tensor_copy(out=xg_s[:], in_=xs[:].indirect(o1[:]))
-        up_sc = tile("up_sc", [P, 2, R], U8)
-        for a in range(2):
+        w_sc = tile("w_sc", [P, R], U8)
+        w2_sc = tile("w2_sc", [P, R], U8)
+
+        def deal_bytes(dst, src):
             nc.vector.tensor_copy(
-                out=up_sc[:, a, :].rearrange("p (t c i) -> p c t i", t=PACK, i=16),
-                in_=up_raw[:, a * R : (a + 1) * R].rearrange("p (c i t) -> p c t i", t=PACK, i=16),
+                out=dst[:].rearrange("p (t c i) -> p c t i", t=PACK, i=16),
+                in_=src[:].rearrange("p (c i t) -> p c t i", t=PACK, i=16),
             )
+
+        spread_split(xs, xs_stage)
+        spread_split(w_sraw, w_stage)
+        nc.vector.tensor_copy(out=xg_s[:], in_=xs[:].indirect(o1[:]))
+        deal_bytes(w_sc, w_sraw)
         nc.vector.tensor_copy(out=xg_w[:], in_=xw[:].indirect(o1[:]))
+        spread_split(w2_sraw, w2_stage)
+        deal_bytes(w2_sc, w2_sraw)
 
         w_p = tile("w_p", [P, 2 * R], U8)
         w2_p = tile("w2_p", [P, R], U32)
@@ -114,7 +138,7 @@ def tile_list_gaintable_twow_further_plain_kernel(
             nc.tensor.matmul_mx(
                 out=a_ps[t // 2][:, t % 2, :],
                 lhsT=w_p[:, 2 * P * t : 2 * P * (t + 1)].bitcast(E2M1),
-                lhsT_scale=up_sc[:, 0, P * t : P * (t + 1)],
+                lhsT_scale=w_sc[:, P * t : P * (t + 1)],
                 rhs=xg_w[:].bitcast(E5M2), rhs_scale=xg_s[:], start=True, stop=True,
             )
         for h in range(2):
@@ -123,7 +147,7 @@ def tile_list_gaintable_twow_further_plain_kernel(
                 nc.tensor.matmul_mx(
                     out=b_ps[h][:, t, :],
                     lhsT=w2_p[:, P * t : P * (t + 1)].bitcast(E4M3),
-                    lhsT_scale=up_sc[:, 1, P * t : P * (t + 1)],
+                    lhsT_scale=w2_sc[:, P * t : P * (t + 1)],
                     rhs=xg_w[:, js].bitcast(E5M2), rhs_scale=xg_s[:, js], start=True, stop=True,
                 )
 

@@ -44,14 +44,21 @@ def tile_list_gaintable_twow_further_plain_kernel(
                 lambda: queue_hi.dma_start(stage[64:68], rows[:, 2:4, :]),
             ]
 
-        def spread_split(plane, stage):
+        def move_rows(plane, q, rows, base, same_partition_copy):
+            dst = plane[32 * q : 32 * q + 4, :]
+            if 32 * q == base:
+                same_partition_copy(out=dst.bitcast(U32), in_=rows.bitcast(U32))
+            else:
+                nc.vector.tensor_copy(out=dst.bitcast(I32), in_=rows)
+
+        def spread_split(plane, stage, same_partition_copy):
             for q in range(4):
                 base = 64 * (q // 2)
-                nc.vector.tensor_copy(out=plane[32 * q : 32 * q + 4, :].bitcast(I32), in_=stage[base : base + 4, q % 2, :])
+                move_rows(plane, q, stage[base : base + 4, q % 2, :], base, same_partition_copy)
 
         def spread(plane, stage):
             for q in range(4):
-                nc.vector.tensor_copy(out=plane[32 * q : 32 * q + 4, :].bitcast(I32), in_=stage[:, q, :])
+                move_rows(plane, q, stage[:, q, :], 0, nc.scalar.copy)
 
         o1 = tile("o1", [P, J // 16], U16)
         o2 = tile("o2", [P, J // 16], U16)
@@ -62,7 +69,7 @@ def tile_list_gaintable_twow_further_plain_kernel(
         w_raw = tile("w_raw", [P, 2 * R], U8)
         w2_raw = tile("w2_raw", [P, R], U32)
         w_stage = tile("w_stage", [P, 2, R // 4], I32)
-        w2_stage = tile("w2_stage", [P, 2, R // 4], I32)
+        w2_stage = tile("w2_stage", [4, 4, R // 4], I32)
         w_sraw = tile("w_sraw", [P, R], U8)
         w2_sraw = tile("w2_sraw", [P, R], U8)
         dn_stage = tile("dn_stage", [4, 4, 2 * N // 4], I32)
@@ -75,22 +82,20 @@ def tile_list_gaintable_twow_further_plain_kernel(
 
         xs_load = load_split(nc.scalar, nc.sync, xs_stage, xt_scales)
         w_load = load_split(nc.sync, nc.sync, w_stage, w_scales)
-        w2_load = load_split(nc.sync, nc.sync, w2_stage, w2_scales)
         nc.sync.dma_start(o1[:], offs)
         xs_load[0]()
         xs_load[1]()
         nc.scalar.dma_start(xw[:].bitcast(I32), xt_words[0].rearrange("p n t -> p (n t)").bitcast(I32))
         w_load[0]()
-        nc.scalar.dma_start(w_raw[:].bitcast(I32), w_words[0].bitcast(I32))
         w_load[1]()
-        nc.scalar.dma_start(w2_raw[:].bitcast(I32), w2_words[0].rearrange("p n t -> p (n t)").bitcast(I32))
+        nc.sync.dma_start(w_raw[:].bitcast(I32), w_words[0].bitcast(I32))
+        nc.sync.dma_start(w2_raw[:].bitcast(I32), w2_words[0].rearrange("p n t -> p (n t)").bitcast(I32))
         nc.sync.dma_start(tbs[0][:], tb_rows[0])
-        w2_load[0]()
-        w2_load[1]()
+        nc.sync.dma_start(o3[:], offs3)
+        nc.sync.dma_start(tbs[1][:], tb_rows[1])
+        nc.sync.dma_start(w2_stage[:], scale_rows(w2_scales))
         nc.sync.dma_start(o2[:], offs2)
         nc.sync.dma_start(st_sb[:], st.rearrange("(p t) o -> p (t o)", t=PACK))
-        nc.sync.dma_start(tbs[1][:], tb_rows[1])
-        nc.sync.dma_start(o3[:], offs3)
         nc.sync.dma_start(tbs[2][:], tb_rows[2])
         nc.sync.dma_start(dn_stage[:, :, 0 : N // 4], scale_rows(ws_scales))
         nc.sync.dma_start(dn_stage[:, :, N // 4 : 2 * N // 4], scale_rows(wb_scales))
@@ -112,13 +117,11 @@ def tile_list_gaintable_twow_further_plain_kernel(
                 in_=src[:].rearrange("p (c i t) -> p c t i", t=PACK, i=16),
             )
 
-        spread_split(xs, xs_stage)
-        spread_split(w_sraw, w_stage)
+        spread_split(xs, xs_stage, nc.vector.tensor_copy)
+        spread_split(w_sraw, w_stage, nc.vector.tensor_copy)
         nc.vector.tensor_copy(out=xg_s[:], in_=xs[:].indirect(o1[:]))
         deal_bytes(w_sc, w_sraw)
         nc.vector.tensor_copy(out=xg_w[:], in_=xw[:].indirect(o1[:]))
-        spread_split(w2_sraw, w2_stage)
-        deal_bytes(w2_sc, w2_sraw)
 
         w_p = tile("w_p", [P, 2 * R], U8)
         w2_p = tile("w2_p", [P, R], U32)
@@ -141,6 +144,13 @@ def tile_list_gaintable_twow_further_plain_kernel(
                 lhsT_scale=w_sc[:, P * t : P * (t + 1)],
                 rhs=xg_w[:].bitcast(E5M2), rhs_scale=xg_s[:], start=True, stop=True,
             )
+
+        x3_s = tile("x3_s", [P, J], U8)
+        x3_w = tile("x3_w", [P, J], U32)
+        nc.vector.tensor_copy(out=x3_s[:], in_=xs[:].indirect(o3[:]))
+        nc.vector.tensor_copy(out=x3_w[:], in_=xw[:].indirect(o3[:]))
+        spread(w2_sraw, w2_stage)
+        deal_bytes(w2_sc, w2_sraw)
         for h in range(2):
             js = slice(h * HALF, (h + 1) * HALF)
             for t in range(PACK):
@@ -151,10 +161,6 @@ def tile_list_gaintable_twow_further_plain_kernel(
                     rhs=xg_w[:, js].bitcast(E5M2), rhs_scale=xg_s[:, js], start=True, stop=True,
                 )
 
-        x3_s = tile("x3_s", [P, J], U8)
-        x3_w = tile("x3_w", [P, J], U32)
-        nc.vector.tensor_copy(out=x3_s[:], in_=xs[:].indirect(o3[:]))
-        nc.vector.tensor_copy(out=x3_w[:], in_=xw[:].indirect(o3[:]))
         spread(dn_sc, dn_stage)
         for h in range(2):
             js = slice(h * HALF, (h + 1) * HALF)
@@ -168,6 +174,18 @@ def tile_list_gaintable_twow_further_plain_kernel(
 
         gains = tile("gains", [P, PACK, J], F32)
         prod = tile("prod", [P, 2, PACK, HALF], F32)
+        hid = [tile("hid%d" % h, [P, HALF, PACK], BF16) for h in range(2)]
+        hq_w = [tile("hq_w%d" % h, [P, HALF], U32) for h in range(2)]
+        hq_s = [tile("hq_s%d" % h, [P, HALF], U8) for h in range(2)]
+
+        def larger(h):
+            nc.vector.tensor_tensor(
+                out=hid[h][:].rearrange("p (c i) t -> p c t i", i=2),
+                in0=b_ps[h][:].rearrange("p t (c i) -> p c t i", i=2),
+                in1=prod[:, h].rearrange("p t (c i) -> p c t i", i=2),
+                op=ALU.max,
+            )
+
         for t in range(PACK - 1):
             nc.scalar.activation(out=gains[:, t, :], in_=tbs[t][:].indirect(o2[:]), func=COPY, scale=st_sb[:, t : t + 1])
             nc.vector.tensor_tensor(
@@ -183,21 +201,10 @@ def tile_list_gaintable_twow_further_plain_kernel(
                 out=gains[:, t, js], in_=tbs[t][:].indirect(o2[:, 8 * h : 8 * (h + 1)]), func=COPY, scale=st_sb[:, t : t + 1]
             )
             nc.vector.tensor_tensor(out=prod[:, h, t, :], in0=a_ps[t // 2][:, t % 2, js], in1=gains[:, t, js], op=ALU.mult)
-
-        hid = [tile("hid%d" % h, [P, HALF, PACK], BF16) for h in range(2)]
-        hq_w = [tile("hq_w%d" % h, [P, HALF], U32) for h in range(2)]
-        hq_s = [tile("hq_s%d" % h, [P, HALF], U8) for h in range(2)]
         for h in range(2):
-            nc.vector.tensor_tensor(
-                out=hid[h][:].rearrange("p (c i) t -> p c t i", i=2),
-                in0=b_ps[h][:].rearrange("p t (c i) -> p c t i", i=2),
-                in1=prod[:, h].rearrange("p t (c i) -> p c t i", i=2),
-                op=ALU.max,
-            )
-        res = [tile("res%d" % h, [P, 2, HALF], F32) for h in range(2)]
-        out_v = out.rearrange("(u p) j -> p u j", p=P)
+            larger(h)
+        res = [[tile("res%d%d" % (h, u), [P, HALF], F32) for u in range(2)] for h in range(2)]
         for h in range(2):
-            js = slice(h * HALF, (h + 1) * HALF)
             nc.vector.quantize_mx(out=hq_w[h][:].bitcast(E4M3), scales=hq_s[h][:], in_=hid[h][:].rearrange("p j t -> p (j t)"))
             for u in range(2):
                 nc.tensor.matmul_mx(
@@ -208,9 +215,10 @@ def tile_list_gaintable_twow_further_plain_kernel(
                 )
         for h in range(2):
             js = slice(h * HALF, (h + 1) * HALF)
-            nc.scalar.copy(out=res[h][:, 0, :], in_=y_ps[h][0][:])
-            if h == 0:
-                nc.scalar.copy(out=res[h][:, 1, :], in_=y_ps[h][1][:])
-            else:
-                nc.vector.tensor_copy(out=res[h][:, 1, :], in_=y_ps[h][1][:])
-            nc.sync.dma_start(out_v[:, :, js], res[h][:])
+            for u in range(2):
+                if (h, u) == (1, 1):
+                    nc.vector.tensor_copy(out=res[h][u][:], in_=y_ps[h][u][:])
+                else:
+                    nc.scalar.copy(out=res[h][u][:], in_=y_ps[h][u][:])
+                queue = nc.scalar if (h, u) == (1, 0) else nc.sync
+                queue.dma_start(out[P * u : P * (u + 1), js], res[h][u][:])

@@ -68,12 +68,8 @@ def tile_list_gaintable_twow_further_plain_kernel(
         xs = tile("xs", [P, T], U8)
         w_raw = tile("w_raw", [P, 2 * R], U8)
         w2_raw = tile("w2_raw", [P, R], U32)
-        w_stage = tile("w_stage", [P, 2, R // 4], I32)
-        w2_stage = tile("w2_stage", [4, 4, R // 4], I32)
-        w_sraw = tile("w_sraw", [P, R], U8)
-        w2_sraw = tile("w2_sraw", [P, R], U8)
-        dn_stage = tile("dn_stage", [4, 4, 2 * N // 4], I32)
-        dn_sc = tile("dn_sc", [P, 2 * N], U8)
+        wt_stage = tile("wt_stage", [4, 4, 384], I32)
+        wt_sc = tile("wt_sc", [P, 1536], U8)
         wb_w = tile("wb_w", [P, 2 * N], U8)
         ws_w = tile("ws_w", [P, 2 * N], U8)
         st_sb = tile("st_sb", [P, PACK], F32)
@@ -81,29 +77,27 @@ def tile_list_gaintable_twow_further_plain_kernel(
         tb_rows = tb.rearrange("(p t) v -> t p v", t=PACK)
 
         xs_load = load_split(nc.scalar, nc.sync, xs_stage, xt_scales)
-        w_load = load_split(nc.sync, nc.sync, w_stage, w_scales)
         nc.sync.dma_start(o1[:], offs)
         xs_load[0]()
         xs_load[1]()
         nc.scalar.dma_start(xw[:].bitcast(I32), xt_words[0].rearrange("p n t -> p (n t)").bitcast(I32))
-        w_load[0]()
-        w_load[1]()
         nc.sync.dma_start(w_raw[:].bitcast(I32), w_words[0].bitcast(I32))
-        nc.sync.dma_start(w2_raw[:].bitcast(I32), w2_words[0].rearrange("p n t -> p (n t)").bitcast(I32))
+        nc.sync.dma_start(wt_stage[:, :, 0:128], scale_rows(w_scales))
+        nc.sync.dma_start(wt_stage[:, :, 128:256], scale_rows(w2_scales))
+        nc.scalar.dma_start(wt_stage[:, :, 256:320], scale_rows(ws_scales))
         nc.sync.dma_start(tbs[0][:], tb_rows[0])
-        nc.sync.dma_start(o3[:], offs3)
+        nc.scalar.dma_start(wt_stage[:, :, 320:384], scale_rows(wb_scales))
         nc.sync.dma_start(tbs[1][:], tb_rows[1])
-        nc.sync.dma_start(w2_stage[:], scale_rows(w2_scales))
+        nc.sync.dma_start(o3[:], offs3)
         nc.sync.dma_start(o2[:], offs2)
         nc.sync.dma_start(st_sb[:], st.rearrange("(p t) o -> p (t o)", t=PACK))
+        nc.sync.dma_start(w2_raw[:].bitcast(I32), w2_words[0].rearrange("p n t -> p (n t)").bitcast(I32))
         nc.sync.dma_start(tbs[2][:], tb_rows[2])
-        nc.sync.dma_start(dn_stage[:, :, 0 : N // 4], scale_rows(ws_scales))
-        nc.sync.dma_start(dn_stage[:, :, N // 4 : 2 * N // 4], scale_rows(wb_scales))
         nc.sync.dma_start(tbs[3][:], tb_rows[3])
         nc.sync.dma_start(ws_w[:].bitcast(I32), ws_words[0].bitcast(I32))
         nc.sync.dma_start(wb_w[:].bitcast(I32), wb_words[0].bitcast(I32))
 
-        for plane in (xs, w_sraw, w2_sraw, dn_sc):
+        for plane in (xs, wt_sc):
             nc.vector.memset(plane[:].bitcast(U32), 0)
 
         xg_s = tile("xg_s", [P, J], U8)
@@ -114,25 +108,22 @@ def tile_list_gaintable_twow_further_plain_kernel(
         def deal_bytes(dst, src):
             nc.vector.tensor_copy(
                 out=dst[:].rearrange("p (t c i) -> p c t i", t=PACK, i=16),
-                in_=src[:].rearrange("p (c i t) -> p c t i", t=PACK, i=16),
+                in_=src.rearrange("p (c i t) -> p c t i", t=PACK, i=16),
             )
 
         spread_split(xs, xs_stage, nc.vector.tensor_copy)
-        spread_split(w_sraw, w_stage, nc.vector.tensor_copy)
         nc.vector.tensor_copy(out=xg_s[:], in_=xs[:].indirect(o1[:]))
-        deal_bytes(w_sc, w_sraw)
         nc.vector.tensor_copy(out=xg_w[:], in_=xw[:].indirect(o1[:]))
-
         w_p = tile("w_p", [P, 2 * R], U8)
         w2_p = tile("w2_p", [P, R], U32)
         nc.scalar.copy(
             out=w_p[:].bitcast(U16).rearrange("p (t c i) -> p c t i", t=PACK, i=8),
             in_=w_raw[:].bitcast(U16).rearrange("p (c i t) -> p c t i", t=PACK, i=8),
         )
-        nc.scalar.copy(
-            out=w2_p[:].rearrange("p (t c i) -> p c t i", t=PACK, i=4),
-            in_=w2_raw[:].rearrange("p (c i t) -> p c t i", t=PACK, i=4),
-        )
+        spread(wt_sc, wt_stage)
+        deal_bytes(w_sc, wt_sc[:, 0:R])
+
+        deal_bytes(w2_sc, wt_sc[:, R : 2 * R])
 
         a_ps = [ps.tile([P, 2, J], F32, name="a%d" % u) for u in range(2)]
         b_ps = [ps.tile([P, PACK, HALF], F32, name="b%d" % h) for h in range(2)]
@@ -149,8 +140,11 @@ def tile_list_gaintable_twow_further_plain_kernel(
         x3_w = tile("x3_w", [P, J], U32)
         nc.vector.tensor_copy(out=x3_s[:], in_=xs[:].indirect(o3[:]))
         nc.vector.tensor_copy(out=x3_w[:], in_=xw[:].indirect(o3[:]))
-        spread(w2_sraw, w2_stage)
-        deal_bytes(w2_sc, w2_sraw)
+        nc.scalar.copy(
+            out=w2_p[:].rearrange("p (t c i) -> p c t i", t=PACK, i=4),
+            in_=w2_raw[:].rearrange("p (c i t) -> p c t i", t=PACK, i=4),
+        )
+
         for h in range(2):
             js = slice(h * HALF, (h + 1) * HALF)
             for t in range(PACK):
@@ -161,14 +155,13 @@ def tile_list_gaintable_twow_further_plain_kernel(
                     rhs=xg_w[:, js].bitcast(E5M2), rhs_scale=xg_s[:, js], start=True, stop=True,
                 )
 
-        spread(dn_sc, dn_stage)
         for h in range(2):
             js = slice(h * HALF, (h + 1) * HALF)
             for u in range(2):
                 nc.tensor.matmul_mx(
                     out=y_ps[h][u][:],
                     lhsT=ws_w[:, 2 * P * u : 2 * P * (u + 1)].bitcast(E2M1),
-                    lhsT_scale=dn_sc[:, P * u : P * (u + 1)],
+                    lhsT_scale=wt_sc[:, 2 * R + P * u : 2 * R + P * (u + 1)],
                     rhs=x3_w[:, js].bitcast(E5M2), rhs_scale=x3_s[:, js], start=True, stop=False,
                 )
 
@@ -210,7 +203,7 @@ def tile_list_gaintable_twow_further_plain_kernel(
                 nc.tensor.matmul_mx(
                     out=y_ps[h][u][:],
                     lhsT=wb_w[:, 2 * P * u : 2 * P * (u + 1)].bitcast(E2M1),
-                    lhsT_scale=dn_sc[:, N + P * u : N + P * (u + 1)],
+                    lhsT_scale=wt_sc[:, 2 * R + N + P * u : 2 * R + N + P * (u + 1)],
                     rhs=hq_w[h][:].bitcast(E4M3), rhs_scale=hq_s[h][:], start=False, stop=True,
                 )
         for h in range(2):

from contextlib import ExitStack

import concourse.mybir as mybir

K, T, J, R, V, N = 512, 1024, 256, 512, 1024, 256
FLOPS = 2 * (2 * K * R * J + R * N * J + K * N * J)

F32 = mybir.dt.float32
BF16 = mybir.dt.bfloat16
I32 = mybir.dt.int32
U32 = mybir.dt.uint32
U16 = mybir.dt.uint16
U8 = mybir.dt.uint8
E4M3 = mybir.dt.float8_e4m3fn_x4
E5M2 = mybir.dt.float8_e5m2_x4
E2M1 = mybir.dt.float4_e2m1fn_x4
ALU = mybir.AluOpType
COPY = mybir.ActivationFunctionType.Copy

P = 128
PACK = 4
HALF = J // 2


def tile_list_gaintable_twow_further_plain_kernel(
    tc, xt_words, xt_scales, w_words, w_scales, w2_words, w2_scales, tb, st,
    wb_words, wb_scales, ws_words, ws_scales, offs, offs2, offs3, out,
):
    nc = tc.nc
    with ExitStack() as ctx:
        sb = ctx.enter_context(tc.tile_pool(name="sb", bufs=1))
        ps = ctx.enter_context(tc.psum_pool(name="ps", bufs=1))

        def tile(name, shape, dtype):
            return sb.tile(shape, dtype, name=name, align_bytes=64)

        def scale_rows(scales):
            return scales[0].bitcast(I32).rearrange("(q r) c -> r q c", r=4)

        def load_split(queue_lo, queue_hi, stage, scales):
            rows = scale_rows(scales)
            return [
                lambda: queue_lo.dma_start(stage[0:4], rows[:, 0:2, :]),
                lambda: queue_hi.dma_start(stage[64:68], rows[:, 2:4, :]),
            ]

        def move_rows(plane, q, rows, base, same_partition_copy):
            dst = plane[32 * q : 32 * q + 4, :]
            if 32 * q == base:
                same_partition_copy(out=dst.bitcast(U32), in_=rows.bitcast(U32))
            else:
                nc.vector.tensor_copy(out=dst.bitcast(I32), in_=rows)

        def spread_split(plane, stage, same_partition_copy):
            for q in range(4):
                base = 64 * (q // 2)
                move_rows(plane, q, stage[base : base + 4, q % 2, :], base, same_partition_copy)

        def spread(plane, stage):
            for q in range(4):
                move_rows(plane, q, stage[:, q, :], 0, nc.scalar.copy)

        o1 = tile("o1", [P, J // 16], U16)
        o2 = tile("o2", [P, J // 16], U16)
        o3 = tile("o3", [P, J // 16], U16)
        xw = tile("xw", [P, T], U32)
        xs_stage = tile("xs_stage", [P, 2, T // 4], I32)
        xs = tile("xs", [P, T], U8)
        w_raw = tile("w_raw", [P, 2 * R], U8)
        w2_raw = tile("w2_raw", [P, R], U32)
        wt_stage = tile("wt_stage", [4, 4, 384], I32)
        wt_sc = tile("wt_sc", [P, 1536], U8)
        wb_w = tile("wb_w", [P, 2 * N], U8)
        ws_w = tile("ws_w", [P, 2 * N], U8)
        st_sb = tile("st_sb", [P, PACK], F32)
        tbs = [tile("tb%d" % t, [P, V], F32) for t in range(PACK)]
        tb_rows = tb.rearrange("(p t) v -> t p v", t=PACK)

        xs_load = load_split(nc.scalar, nc.sync, xs_stage, xt_scales)
        nc.sync.dma_start(o1[:], offs)
        xs_load[0]()
        xs_load[1]()
        nc.scalar.dma_start(xw[:].bitcast(I32), xt_words[0].rearrange("p n t -> p (n t)").bitcast(I32))
        nc.sync.dma_start(w_raw[:].bitcast(I32), w_words[0].bitcast(I32))
        nc.sync.dma_start(wt_stage[:, :, 0:128], scale_rows(w_scales))
        nc.sync.dma_start(wt_stage[:, :, 128:256], scale_rows(w2_scales))
        nc.scalar.dma_start(wt_stage[:, :, 256:320], scale_rows(ws_scales))
        nc.sync.dma_start(tbs[0][:], tb_rows[0])
        nc.scalar.dma_start(wt_stage[:, :, 320:384], scale_rows(wb_scales))
        nc.sync.dma_start(tbs[1][:], tb_rows[1])
        nc.sync.dma_start(o3[:], offs3)
        nc.sync.dma_start(o2[:], offs2)
        nc.sync.dma_start(st_sb[:], st.rearrange("(p t) o -> p (t o)", t=PACK))
        nc.sync.dma_start(w2_raw[:].bitcast(I32), w2_words[0].rearrange("p n t -> p (n t)").bitcast(I32))
        nc.sync.dma_start(tbs[2][:], tb_rows[2])
        nc.sync.dma_start(tbs[3][:], tb_rows[3])
        nc.sync.dma_start(ws_w[:].bitcast(I32), ws_words[0].bitcast(I32))
        nc.sync.dma_start(wb_w[:].bitcast(I32), wb_words[0].bitcast(I32))

        for plane in (xs, wt_sc):
            nc.vector.memset(plane[:].bitcast(U32), 0)

        xg_s = tile("xg_s", [P, J], U8)
        xg_w = tile("xg_w", [P, J], U32)
        w_sc = tile("w_sc", [P, R], U8)
        w2_sc = tile("w2_sc", [P, R], U8)

        def deal_bytes(dst, src):
            nc.vector.tensor_copy(
                out=dst[:].rearrange("p (t c i) -> p c t i", t=PACK, i=16),
                in_=src.rearrange("p (c i t) -> p c t i", t=PACK, i=16),
            )

        spread_split(xs, xs_stage, nc.vector.tensor_copy)
        nc.vector.tensor_copy(out=xg_s[:], in_=xs[:].indirect(o1[:]))
        nc.vector.tensor_copy(out=xg_w[:], in_=xw[:].indirect(o1[:]))
        w_p = tile("w_p", [P, 2 * R], U8)
        w2_p = tile("w2_p", [P, R], U32)
        nc.scalar.copy(
            out=w_p[:].bitcast(U16).rearrange("p (t c i) -> p c t i", t=PACK, i=8),
            in_=w_raw[:].bitcast(U16).rearrange("p (c i t) -> p c t i", t=PACK, i=8),
        )
        spread(wt_sc, wt_stage)
        deal_bytes(w_sc, wt_sc[:, 0:R])

        deal_bytes(w2_sc, wt_sc[:, R : 2 * R])

        a_ps = [ps.tile([P, 2, J], F32, name="a%d" % u) for u in range(2)]
        b_ps = [ps.tile([P, PACK, HALF], F32, name="b%d" % h) for h in range(2)]
        y_ps = [[ps.tile([P, HALF], F32, name="y%d%d" % (h, u)) for u in range(2)] for h in range(2)]
        for t in range(PACK):
            nc.tensor.matmul_mx(
                out=a_ps[t // 2][:, t % 2, :],
                lhsT=w_p[:, 2 * P * t : 2 * P * (t + 1)].bitcast(E2M1),
                lhsT_scale=w_sc[:, P * t : P * (t + 1)],
                rhs=xg_w[:].bitcast(E5M2), rhs_scale=xg_s[:], start=True, stop=True,
            )

        x3_s = tile("x3_s", [P, J], U8)
        x3_w = tile("x3_w", [P, J], U32)
        nc.vector.tensor_copy(out=x3_s[:], in_=xs[:].indirect(o3[:]))
        nc.vector.tensor_copy(out=x3_w[:], in_=xw[:].indirect(o3[:]))
        nc.scalar.copy(
            out=w2_p[:].rearrange("p (t c i) -> p c t i", t=PACK, i=4),
            in_=w2_raw[:].rearrange("p (c i t) -> p c t i", t=PACK, i=4),
        )

        for h in range(2):
            js = slice(h * HALF, (h + 1) * HALF)
            for t in range(PACK):
                nc.tensor.matmul_mx(
                    out=b_ps[h][:, t, :],
                    lhsT=w2_p[:, P * t : P * (t + 1)].bitcast(E4M3),
                    lhsT_scale=w2_sc[:, P * t : P * (t + 1)],
                    rhs=xg_w[:, js].bitcast(E5M2), rhs_scale=xg_s[:, js], start=True, stop=True,
                )

        for h in range(2):
            js = slice(h * HALF, (h + 1) * HALF)
            for u in range(2):
                nc.tensor.matmul_mx(
                    out=y_ps[h][u][:],
                    lhsT=ws_w[:, 2 * P * u : 2 * P * (u + 1)].bitcast(E2M1),
                    lhsT_scale=wt_sc[:, 2 * R + P * u : 2 * R + P * (u + 1)],
                    rhs=x3_w[:, js].bitcast(E5M2), rhs_scale=x3_s[:, js], start=True, stop=False,
                )

        gains = tile("gains", [P, PACK, J], F32)
        prod = tile("prod", [P, 2, PACK, HALF], F32)
        hid = [tile("hid%d" % h, [P, HALF, PACK], BF16) for h in range(2)]
        hq_w = [tile("hq_w%d" % h, [P, HALF], U32) for h in range(2)]
        hq_s = [tile("hq_s%d" % h, [P, HALF], U8) for h in range(2)]

        def larger(h):
            nc.vector.tensor_tensor(
                out=hid[h][:].rearrange("p (c i) t -> p c t i", i=2),
                in0=b_ps[h][:].rearrange("p t (c i) -> p c t i", i=2),
                in1=prod[:, h].rearrange("p t (c i) -> p c t i", i=2),
                op=ALU.max,
            )

        for t in range(PACK - 1):
            nc.scalar.activation(out=gains[:, t, :], in_=tbs[t][:].indirect(o2[:]), func=COPY, scale=st_sb[:, t : t + 1])
            nc.vector.tensor_tensor(
                out=prod[:, :, t, :],
                in0=a_ps[t // 2][:, t % 2, :].rearrange("p (h j) -> p h j", h=2),
                in1=gains[:, t, :].rearrange("p (h j) -> p h j", h=2),
                op=ALU.mult,
            )
        t = PACK - 1
        for h in range(2):
            js = slice(h * HALF, (h + 1) * HALF)
            nc.scalar.activation(
                out=gains[:, t, js], in_=tbs[t][:].indirect(o2[:, 8 * h : 8 * (h + 1)]), func=COPY, scale=st_sb[:, t : t + 1]
            )
            nc.vector.tensor_tensor(out=prod[:, h, t, :], in0=a_ps[t // 2][:, t % 2, js], in1=gains[:, t, js], op=ALU.mult)
        for h in range(2):
            larger(h)
        res = [[tile("res%d%d" % (h, u), [P, HALF], F32) for u in range(2)] for h in range(2)]
        for h in range(2):
            nc.vector.quantize_mx(out=hq_w[h][:].bitcast(E4M3), scales=hq_s[h][:], in_=hid[h][:].rearrange("p j t -> p (j t)"))
            for u in range(2):
                nc.tensor.matmul_mx(
                    out=y_ps[h][u][:],
                    lhsT=wb_w[:, 2 * P * u : 2 * P * (u + 1)].bitcast(E2M1),
                    lhsT_scale=wt_sc[:, 2 * R + N + P * u : 2 * R + N + P * (u + 1)],
                    rhs=hq_w[h][:].bitcast(E4M3), rhs_scale=hq_s[h][:], start=False, stop=True,
                )
        for h in range(2):
            js = slice(h * HALF, (h + 1) * HALF)
            for u in range(2):
                if (h, u) == (1, 1):
                    nc.vector.tensor_copy(out=res[h][u][:], in_=y_ps[h][u][:])
                else:
                    nc.scalar.copy(out=res[h][u][:], in_=y_ps[h][u][:])
                queue = nc.scalar if (h, u) == (1, 0) else nc.sync
                queue.dma_start(out[P * u : P * (u + 1), js], res[h][u][:])
